import numpy as np
import ml_dtypes


def mxq(x, axis, fmt="e4m3"):
    dtype, down = {"e4m3": (ml_dtypes.float8_e4m3fn, 7), "e5m2": (ml_dtypes.float8_e5m2, 14)}[fmt]
    v = np.moveaxis(np.asarray(x, np.float32).astype(ml_dtypes.bfloat16).astype(np.float64), axis, -1)
    blocks = v.reshape(v.shape[:-1] + (-1, 32))
    amax = np.abs(blocks).max(-1, keepdims=True)
    byte = np.maximum(np.where(amax > 0, np.frexp(amax)[1] - 1 + 127, 0) - down, 1)
    scale = np.exp2(byte - 127.0)
    codes = (blocks / scale).astype(np.float32).astype(dtype).astype(np.float64)
    return np.moveaxis((codes * scale).reshape(v.shape), -1, axis)


WIDE = False


def mx_kscale(k):
    if not WIDE:
        return np.ones(k)
    levels = np.array([10, -10, 5, -5, 0])
    if k % 512:
        return np.exp2(np.random.permutation(np.resize(levels, k // 32))).repeat(32)
    a = np.empty((k // 512, 16))
    for p in range(k // 512):
        a[p, :8] = np.random.permutation(np.resize(levels, 8))
        for g in range(8):
            far = levels[np.abs(levels - a[p, g]) >= 10]
            a[p, g + 8] = far[np.random.randint(len(far))]
    return np.exp2(a.ravel()).repeat(32)


def f64(x):
    return np.asarray(x).astype(np.float64)


def striped(idx):
    return np.tile(idx.reshape(-1, 16).T, (8, 1)).astype(np.uint16)


def unstriped(offs):
    return offs[:16].T.reshape(-1).astype(np.int64)


def relu(v):
    return np.maximum(v, 0.0)


K, T, S, N = 1024, 1024, 512, 512


def setup_inputs():
    n = np.random.standard_normal
    s = mx_kscale(K)[:, None]
    w1, w2 = n((2, K, N)) / np.sqrt(2 * K) / s[None]
    return {
        "xT": (n((K, S)) * s).astype(np.float32),
        "sT": (n((K, T)) * s).astype(np.float32),
        "w1": w1.astype(np.float32),
        "w2": w2.astype(np.float32),
        "b": (0.3 * n((N, 1))).astype(np.float32),
        "offs": striped(np.random.permutation(T)[:S]),
    }


def reference(xT, sT, w1, w2, b, offs):
    y = mxq(f64(w1), 0, "e4m3").T @ mxq(f64(xT), 0, "e4m3") + mxq(f64(w2), 0, "e4m3").T @ mxq(f64(sT)[:, unstriped(offs)], 0, "e4m3")
    return relu(y + f64(b))

@@ -1,0 +1,153 @@
+from contextlib import ExitStack
+
+import concourse.mybir as mybir
+
+K, T, S, N = 1024, 1024, 512, 512
+FLOPS = 2 * N * S * 2 * K
+
+F32 = mybir.dt.float32
+BF16 = mybir.dt.bfloat16
+U32 = mybir.dt.uint32
+U16 = mybir.dt.uint16
+U8 = mybir.dt.uint8
+FP8X4 = mybir.dt.float8_e4m3fn_x4
+COPY = mybir.ActivationFunctionType.Copy
+RELU = mybir.ActivationFunctionType.Relu
+ADD = mybir.AluOpType.add
+MAX = mybir.AluOpType.max
+
+P = 128
+PACK = 4
+K_PASS = P * PACK
+PASSES = K // K_PASS
+M_TILES = N // P
+
+
+def tile_picked_recall_relu_e_kernel(tc, xT, sT, w1, w2, b, offs, out):
+    nc = tc.nc
+    with ExitStack() as ctx:
+        keep = ctx.enter_context(tc.tile_pool(name="keep", bufs=1))
+        psum = ctx.enter_context(tc.psum_pool(name="psum", bufs=1))
+
+        offsets = keep.tile([P, S // 16], U16, name="offsets")
+
+        def load(src, c, c0, c1, name):
+            raw = keep.tile([P, PACK, c1 - c0], F32, name="raw_" + name)
+            rows = src[c * K_PASS : (c + 1) * K_PASS, c0:c1]
+            nc.sync.dma_start(out=raw[:], in_=rows.rearrange("(p j) w -> p j w", j=PACK))
+            return raw
+
+        b_rows = keep.tile([P, 32], F32, name="b_rows", align_bytes=64)
+        nc.vector.memset(b_rows[:], 0.0)
+
+        raw_x = [load(xT, 0, 0, S, "x0")]
+        raw_s0 = load(sT, 0, 0, T, "s0")
+        nc.sync.dma_start(out=offsets[:], in_=offs)
+        for g in range(4):
+            nc.scalar.dma_start(
+                out=b_rows[32 * g : 32 * g + M_TILES, :],
+                in_=b.rearrange("(c g r) o -> g c (r o)", g=4, r=32)[g],
+            )
+        raw_s1 = load(sT, 1, 0, T, "s1")
+        raw_w2 = [load(w2, c, 0, N, "w2%d" % c) for c in range(PASSES)]
+        raw_x.append(load(xT, 1, 0, S, "x1"))
+        raw_w1 = [load(w1, 0, 0, N, "w10")]
+        raw_w1a = load(w1, 1, 0, 256, "w11a")
+        raw_w1b = load(w1, 1, 256, 512, "w11b")
+
+        def interleave(raw, c0, c1, cut, name, tag=None):
+            grouped = keep.tile([P, c1 - c0, PACK], BF16, name="grouped_" + name, tag=tag or "grouped_" + name, align_bytes=64)
+            nc.vector.tensor_copy(
+                out=grouped[:, :cut, :], in_=raw[:, :, c0 : c0 + cut].rearrange("p j w -> p w j")
+            )
+            nc.scalar.activation(
+                grouped[:, cut:, :], raw[:, :, c0 + cut : c1].rearrange("p j w -> p w j"), COPY
+            )
+            return grouped
+
+        def quantize(grouped, name):
+            width = grouped.shape[1]
+            codes = keep.tile([P, width], U32, name="codes_" + name, align_bytes=64)
+            scales = keep.tile([P, width], U8, name="scales_" + name, align_bytes=64)
+            nc.vector.quantize_mx(
+                out=codes[:].bitcast(FP8X4),
+                scales=scales[:],
+                in_=grouped[:].rearrange("p w j -> p (w j)"),
+            )
+            return codes, scales[:]
+
+        store_scales = keep.tile([P, T], U8, name="store_scales", align_bytes=64)
+        nc.gpsimd.memset(store_scales[:], 0)
+
+        def quantize_store(grouped, c, name):
+            codes = keep.tile([P, T], U32, name="codes_" + name, align_bytes=64)
+            for t0 in range(0, T, 512):
+                cols = slice(t0, t0 + 512)
+                nc.vector.quantize_mx(
+                    out=codes[:, cols].bitcast(FP8X4),
+                    scales=store_scales[4 * c :, cols],
+                    in_=grouped[:, cols, :].rearrange("p w j -> p (w j)"),
+                )
+            return codes
+
+        def gather_words(codes, name):
+            words = keep.tile([P, S], U32, name="words_" + name, align_bytes=64)
+            nc.vector.tensor_copy(words[:], codes[:].indirect(offsets[:]))
+            return words
+
+        acc = [psum.tile([P, S], F32, name="acc%d" % m) for m in range(M_TILES)]
+
+        def multiply(m, weights, cols, moving, start, stop):
+            w_codes, w_scales = weights
+            codes, scales = moving
+            nc.tensor.matmul_mx(
+                out=acc[m][:],
+                lhsT=w_codes[:, cols].bitcast(FP8X4),
+                lhsT_scale=w_scales[:, cols],
+                rhs=codes[:].bitcast(FP8X4),
+                rhs_scale=scales,
+                start=start,
+                stop=stop,
+            )
+
+        g_x0 = interleave(raw_x[0], 0, S, 192, "x0")
+        g_s0 = interleave(raw_s0, 0, T, 256, "s0")
+        q_x0 = quantize(g_x0, "x0")
+        g_s1 = interleave(raw_s1, 0, T, 256, "s1", tag="bias_after_s1")
+        q_s0 = quantize_store(g_s0, 0, "s0")
+        p_s0 = gather_words(q_s0, "s0")
+        g_w20 = interleave(raw_w2[0], 0, N, 192, "w20")
+        q_s1 = quantize_store(g_s1, 1, "s1")
+        p_s1 = gather_words(q_s1, "s1")
+        picked_scales = keep.tile([P, S], U8, name="picked_scales", align_bytes=64)
+        nc.vector.tensor_copy(picked_scales[:], store_scales[:].indirect(offsets[:]))
+        p_s0 = (p_s0, picked_scales[:])
+        p_s1 = (p_s1, picked_scales[4:, :])
+        b_cols = keep.tile([P, 32], F32, name="b_cols", tag="bias_after_s1", align_bytes=64)
+        nc.vector.transpose(b_cols[:], b_rows[:])
+        g_w21 = interleave(raw_w2[1], 0, N, 192, "w21")
+        q_w20 = quantize(g_w20, "w20")
+        q_w21 = quantize(g_w21, "w21")
+        for m in range(M_TILES):
+            multiply(m, q_w20, slice(m * P, (m + 1) * P), p_s0, True, False)
+        for m in range(M_TILES):
+            multiply(m, q_w21, slice(m * P, (m + 1) * P), p_s1, False, False)
+        g_x1 = interleave(raw_x[1], 0, S, 192, "x1")
+        g_w10 = interleave(raw_w1[0], 0, N, 192, "w10")
+        q_x1 = quantize(g_x1, "x1")
+        q_w10 = quantize(g_w10, "w10")
+        for m in range(M_TILES):
+            multiply(m, q_w10, slice(m * P, (m + 1) * P), q_x0, False, False)
+
+        for h, raw in enumerate((raw_w1a, raw_w1b)):
+            grouped = [interleave(raw, i * P, (i + 1) * P, 84, "w11%d%d" % (h, i)) for i in range(2)]
+            for i in range(2):
+                m = 2 * h + i
+                q_w11 = quantize(grouped[i], "w11%d%d" % (h, i))
+                multiply(m, q_w11, slice(0, P), q_x1, False, True)
+                result = keep.tile([P, S], F32, name="result%d" % m)
+                if i == 0:
+                    nc.scalar.activation(result[:], acc[m][:], RELU, bias=b_cols[:, m : m + 1])
+                else:
+                    nc.vector.tensor_scalar(result[:], acc[m][:], b_cols[:, m : m + 1], 0.0, ADD, MAX)
+                nc.sync.dma_start(out=out[m * P : (m + 1) * P, :], in_=result[:])

@@ -57,12 +57,19 @@ def tile_picked_recall_relu_e_kernel(tc, xT, sT, w1, w2, b, offs, out):
 
         def interleave(raw, c0, c1, cut, name, tag=None):
             grouped = keep.tile([P, c1 - c0, PACK], BF16, name="grouped_" + name, tag=tag or "grouped_" + name, align_bytes=64)
-            nc.vector.tensor_copy(
-                out=grouped[:, :cut, :], in_=raw[:, :, c0 : c0 + cut].rearrange("p j w -> p w j")
-            )
-            nc.scalar.activation(
-                grouped[:, cut:, :], raw[:, :, c0 + cut : c1].rearrange("p j w -> p w j"), COPY
-            )
+            step = min(c1 - c0, 512)
+            for w in range(0, c1 - c0, step):
+                if cut > 0:
+                    nc.vector.tensor_copy(
+                        out=grouped[:, w : w + cut, :].rearrange("p (c i) j -> p c j i", i=4),
+                        in_=raw[:, :, c0 + w : c0 + w + cut].rearrange("p j (c i) -> p c j i", i=4),
+                    )
+                if cut < step:
+                    nc.scalar.activation(
+                        grouped[:, w + cut : w + step, :].rearrange("p (c i) j -> p c j i", i=4),
+                        raw[:, :, c0 + w + cut : c0 + w + step].rearrange("p j (c i) -> p c j i", i=4),
+                        COPY,
+                    )
             return grouped
 
         def quantize(grouped, name):
@@ -110,13 +117,13 @@ def tile_picked_recall_relu_e_kernel(tc, xT, sT, w1, w2, b, offs, out):
                 stop=stop,
             )
 
-        g_x0 = interleave(raw_x[0], 0, S, 192, "x0")
+        g_x0 = interleave(raw_x[0], 0, S, 152, "x0")
         g_s0 = interleave(raw_s0, 0, T, 256, "s0")
         q_x0 = quantize(g_x0, "x0")
         g_s1 = interleave(raw_s1, 0, T, 256, "s1", tag="bias_after_s1")
         q_s0 = quantize_store(g_s0, 0, "s0")
         p_s0 = gather_words(q_s0, "s0")
-        g_w20 = interleave(raw_w2[0], 0, N, 192, "w20")
+        g_w20 = interleave(raw_w2[0], 0, N, 152, "w20")
         q_s1 = quantize_store(g_s1, 1, "s1")
         p_s1 = gather_words(q_s1, "s1")
         picked_scales = keep.tile([P, S], U8, name="picked_scales", align_bytes=64)
@@ -125,28 +132,29 @@ def tile_picked_recall_relu_e_kernel(tc, xT, sT, w1, w2, b, offs, out):
         p_s1 = (p_s1, picked_scales[4:, :])
         b_cols = keep.tile([P, 32], F32, name="b_cols", tag="bias_after_s1", align_bytes=64)
         nc.vector.transpose(b_cols[:], b_rows[:])
-        g_w21 = interleave(raw_w2[1], 0, N, 192, "w21")
+        g_w21 = interleave(raw_w2[1], 0, N, 152, "w21")
         q_w20 = quantize(g_w20, "w20")
         q_w21 = quantize(g_w21, "w21")
         for m in range(M_TILES):
             multiply(m, q_w20, slice(m * P, (m + 1) * P), p_s0, True, False)
         for m in range(M_TILES):
             multiply(m, q_w21, slice(m * P, (m + 1) * P), p_s1, False, False)
-        g_x1 = interleave(raw_x[1], 0, S, 192, "x1")
-        g_w10 = interleave(raw_w1[0], 0, N, 192, "w10")
+        g_x1 = interleave(raw_x[1], 0, S, 152, "x1")
+        g_w10 = interleave(raw_w1[0], 0, N, 152, "w10")
         q_x1 = quantize(g_x1, "x1")
         q_w10 = quantize(g_w10, "w10")
         for m in range(M_TILES):
             multiply(m, q_w10, slice(m * P, (m + 1) * P), q_x0, False, False)
 
         for h, raw in enumerate((raw_w1a, raw_w1b)):
-            grouped = [interleave(raw, i * P, (i + 1) * P, 84, "w11%d%d" % (h, i)) for i in range(2)]
+            cuts = (128, 0) if h == 0 else (128, 128)
+            grouped = [interleave(raw, i * P, (i + 1) * P, cuts[i], "w11%d%d" % (h, i)) for i in range(2)]
             for i in range(2):
                 m = 2 * h + i
                 q_w11 = quantize(grouped[i], "w11%d%d" % (h, i))
                 multiply(m, q_w11, slice(0, P), q_x1, False, True)
                 result = keep.tile([P, S], F32, name="result%d" % m)
-                if i == 0:
+                if m != 2:
                     nc.scalar.activation(result[:], acc[m][:], RELU, bias=b_cols[:, m : m + 1])
                 else:
                     nc.vector.tensor_scalar(result[:], acc[m][:], b_cols[:, m : m + 1], 0.0, ADD, MAX)

@@ -30,47 +30,28 @@ def tile_picked_recall_relu_e_kernel(tc, xT, sT, w1, w2, b, offs, out):
         psum = ctx.enter_context(tc.psum_pool(name="psum", bufs=1))
 
         offsets = keep.tile([P, S // 16], U16, name="offsets")
-
-        def load(src, c, c0, c1, name):
-            raw = keep.tile([P, PACK, c1 - c0], F32, name="raw_" + name)
-            rows = src[c * K_PASS : (c + 1) * K_PASS, c0:c1]
-            nc.sync.dma_start(out=raw[:], in_=rows.rearrange("(p j) w -> p j w", j=PACK))
-            return raw
-
         b_rows = keep.tile([P, 32], F32, name="b_rows", align_bytes=64)
         nc.vector.memset(b_rows[:], 0.0)
 
-        raw_x = [load(xT, 0, 0, S, "x0")]
-        raw_s0 = load(sT, 0, 0, T, "s0")
-        nc.sync.dma_start(out=offsets[:], in_=offs)
-        for g in range(4):
-            nc.scalar.dma_start(
-                out=b_rows[32 * g : 32 * g + M_TILES, :],
-                in_=b.rearrange("(c g r) o -> g c (r o)", g=4, r=32)[g],
-            )
-        raw_s1 = load(sT, 1, 0, T, "s1")
-        raw_w2 = [load(w2, c, 0, N, "w2%d" % c) for c in range(PASSES)]
-        raw_x.append(load(xT, 1, 0, S, "x1"))
-        raw_w1 = [load(w1, 0, 0, N, "w10")]
-        raw_w1a = load(w1, 1, 0, 256, "w11a")
-        raw_w1b = load(w1, 1, 256, 512, "w11b")
+        def load(src, c, j0, j1, c0, c1, name):
+            raw = keep.tile([P, j1 - j0, c1 - c0], F32, name="raw_" + name)
+            rows = src[c * K_PASS : (c + 1) * K_PASS, c0:c1].rearrange("(p j) w -> p j w", j=PACK)
+            nc.sync.dma_start(out=raw[:], in_=rows[:, j0:j1, :])
+            return raw
 
-        def interleave(raw, c0, c1, cut, name, tag=None):
-            grouped = keep.tile([P, c1 - c0, PACK], BF16, name="grouped_" + name, tag=tag or "grouped_" + name, align_bytes=64)
-            step = min(c1 - c0, 512)
-            for w in range(0, c1 - c0, step):
-                if cut > 0:
-                    nc.vector.tensor_copy(
-                        out=grouped[:, w : w + cut, :].rearrange("p (c i) j -> p c j i", i=4),
-                        in_=raw[:, :, c0 + w : c0 + w + cut].rearrange("p j (c i) -> p c j i", i=4),
-                    )
-                if cut < step:
-                    nc.scalar.activation(
-                        grouped[:, w + cut : w + step, :].rearrange("p (c i) j -> p c j i", i=4),
-                        raw[:, :, c0 + w + cut : c0 + w + step].rearrange("p j (c i) -> p c j i", i=4),
-                        COPY,
-                    )
-            return grouped
+        def interleave(grouped, raw, cut):
+            width = raw.shape[2]
+            if cut > 0:
+                nc.vector.tensor_copy(
+                    out=grouped[:, :cut, :].rearrange("p (c i) j -> p c j i", i=4),
+                    in_=raw[:, :, :cut].rearrange("p j (c i) -> p c j i", i=4),
+                )
+            if cut < width:
+                nc.scalar.activation(
+                    grouped[:, cut:, :].rearrange("p (c i) j -> p c j i", i=4),
+                    raw[:, :, cut:].rearrange("p j (c i) -> p c j i", i=4),
+                    COPY,
+                )
 
         def quantize(grouped, name):
             width = grouped.shape[1]
@@ -81,74 +62,75 @@ def tile_picked_recall_relu_e_kernel(tc, xT, sT, w1, w2, b, offs, out):
                 scales=scales[:],
                 in_=grouped[:].rearrange("p w j -> p (w j)"),
             )
-            return codes, scales[:]
+            return codes, scales
 
-        store_scales = keep.tile([P, T], U8, name="store_scales", align_bytes=64)
-        nc.gpsimd.memset(store_scales[:], 0)
+        def dense(raw, name, cut):
+            grouped = keep.tile([P, raw.shape[2], PACK], BF16, name="grouped_" + name, align_bytes=64)
+            interleave(grouped, raw, cut)
+            return quantize(grouped, name)
 
-        def quantize_store(grouped, c, name):
-            codes = keep.tile([P, T], U32, name="codes_" + name, align_bytes=64)
-            for t0 in range(0, T, 512):
-                cols = slice(t0, t0 + 512)
-                nc.vector.quantize_mx(
-                    out=codes[:, cols].bitcast(FP8X4),
-                    scales=store_scales[4 * c :, cols],
-                    in_=grouped[:, cols, :].rearrange("p w j -> p (w j)"),
-                )
-            return codes
+        def picked_pass(raws, name, cut, tag):
+            grouped = keep.tile([P, S, PACK], BF16, name="picked_" + name, tag=tag, align_bytes=64)
+            words = grouped[:].rearrange("p s j -> p (s j)").bitcast(U32).rearrange("p (s u) -> p s u", u=2)
+            for u in range(2):
+                pairs = keep.tile([P, T, 2], BF16, name="pairs_%s%d" % (name, u), align_bytes=64)
+                interleave(pairs, raws[u], cut)
+                table = pairs[:].rearrange("p t e -> p (t e)").bitcast(U32)
+                nc.vector.tensor_copy(words[:, :, u], table.indirect(offsets[:]))
+            return quantize(grouped, name)
 
-        def gather_words(codes, name):
-            words = keep.tile([P, S], U32, name="words_" + name, align_bytes=64)
-            nc.vector.tensor_copy(words[:], codes[:].indirect(offsets[:]))
-            return words
+        raw_s0 = [load(sT, 0, 0, 2, 0, T, "s00")]
+        nc.sync.dma_start(out=offsets[:], in_=offs)
+        for g in range(4):
+            nc.scalar.dma_start(
+                out=b_rows[32 * g : 32 * g + M_TILES, :],
+                in_=b.rearrange("(c g r) o -> g c (r o)", g=4, r=32)[g],
+            )
+        raw_s0.append(load(sT, 0, 2, 4, 0, T, "s01"))
+        raw_s1 = [load(sT, 1, 2 * u, 2 * u + 2, 0, T, "s1%d" % u) for u in range(2)]
+        raw_w20 = load(w2, 0, 0, 4, 0, N, "w20")
+        raw_x0 = load(xT, 0, 0, 4, 0, S, "x0")
+        raw_w10 = load(w1, 0, 0, 4, 0, N, "w10")
+        raw_w21 = load(w2, 1, 0, 4, 0, N, "w21")
+        raw_x1 = load(xT, 1, 0, 4, 0, S, "x1")
+        raw_w11 = [load(w1, 1, 0, 4, h * 256, (h + 1) * 256, "w11%d" % h) for h in range(2)]
 
         acc = [psum.tile([P, S], F32, name="acc%d" % m) for m in range(M_TILES)]
 
         def multiply(m, weights, cols, moving, start, stop):
-            w_codes, w_scales = weights
-            codes, scales = moving
             nc.tensor.matmul_mx(
                 out=acc[m][:],
-                lhsT=w_codes[:, cols].bitcast(FP8X4),
-                lhsT_scale=w_scales[:, cols],
-                rhs=codes[:].bitcast(FP8X4),
-                rhs_scale=scales,
+                lhsT=weights[0][:, cols].bitcast(FP8X4),
+                lhsT_scale=weights[1][:, cols],
+                rhs=moving[0][:].bitcast(FP8X4),
+                rhs_scale=moving[1][:],
                 start=start,
                 stop=stop,
             )
 
-        g_x0 = interleave(raw_x[0], 0, S, 152, "x0")
-        g_s0 = interleave(raw_s0, 0, T, 256, "s0")
-        q_x0 = quantize(g_x0, "x0")
-        g_s1 = interleave(raw_s1, 0, T, 256, "s1", tag="bias_after_s1")
-        q_s0 = quantize_store(g_s0, 0, "s0")
-        p_s0 = gather_words(q_s0, "s0")
-        g_w20 = interleave(raw_w2[0], 0, N, 152, "w20")
-        q_s1 = quantize_store(g_s1, 1, "s1")
-        p_s1 = gather_words(q_s1, "s1")
-        picked_scales = keep.tile([P, S], U8, name="picked_scales", align_bytes=64)
-        nc.vector.tensor_copy(picked_scales[:], store_scales[:].indirect(offsets[:]))
-        p_s0 = (p_s0, picked_scales[:])
-        p_s1 = (p_s1, picked_scales[4:, :])
-        b_cols = keep.tile([P, 32], F32, name="b_cols", tag="bias_after_s1", align_bytes=64)
+        q_s0 = picked_pass(raw_s0, "s0", 320, "picked_s0")
+        q_s1 = picked_pass(raw_s1, "s1", 320, "picked_s1")
+        b_cols = keep.tile([P, 32], F32, name="b_cols", tag="picked_s1", align_bytes=64)
         nc.vector.transpose(b_cols[:], b_rows[:])
-        g_w21 = interleave(raw_w2[1], 0, N, 152, "w21")
-        q_w20 = quantize(g_w20, "w20")
-        q_w21 = quantize(g_w21, "w21")
+        q_w20 = dense(raw_w20, "w20", 200)
         for m in range(M_TILES):
-            multiply(m, q_w20, slice(m * P, (m + 1) * P), p_s0, True, False)
-        for m in range(M_TILES):
-            multiply(m, q_w21, slice(m * P, (m + 1) * P), p_s1, False, False)
-        g_x1 = interleave(raw_x[1], 0, S, 152, "x1")
-        g_w10 = interleave(raw_w1[0], 0, N, 152, "w10")
-        q_x1 = quantize(g_x1, "x1")
-        q_w10 = quantize(g_w10, "w10")
+            multiply(m, q_w20, slice(m * P, (m + 1) * P), q_s0, True, False)
+        q_x0 = dense(raw_x0, "x0", 200)
+        q_w10 = dense(raw_w10, "w10", 200)
         for m in range(M_TILES):
             multiply(m, q_w10, slice(m * P, (m + 1) * P), q_x0, False, False)
+        q_w21 = dense(raw_w21, "w21", 232)
+        for m in range(M_TILES):
+            multiply(m, q_w21, slice(m * P, (m + 1) * P), q_s1, False, False)
+        q_x1 = dense(raw_x1, "x1", 320)
 
-        for h, raw in enumerate((raw_w1a, raw_w1b)):
+        for h in range(2):
             cuts = (128, 0) if h == 0 else (128, 128)
-            grouped = [interleave(raw, i * P, (i + 1) * P, cuts[i], "w11%d%d" % (h, i)) for i in range(2)]
+            grouped = []
+            for i in range(2):
+                part = keep.tile([P, P, PACK], BF16, name="grouped_w11%d%d" % (h, i), align_bytes=64)
+                interleave(part, raw_w11[h][:, :, i * P : (i + 1) * P], cuts[i])
+                grouped.append(part)
             for i in range(2):
                 m = 2 * h + i
                 q_w11 = quantize(grouped[i], "w11%d%d" % (h, i))

@@ -108,21 +108,21 @@ def tile_picked_recall_relu_e_kernel(tc, xT, sT, w1, w2, b, offs, out):
                 stop=stop,
             )
 
-        q_s0 = picked_pass(raw_s0, "s0", 320, "picked_s0")
-        q_s1 = picked_pass(raw_s1, "s1", 320, "picked_s1")
+        q_s0 = picked_pass(raw_s0, "s0", 256, "picked_s0")
+        q_s1 = picked_pass(raw_s1, "s1", 256, "picked_s1")
         b_cols = keep.tile([P, 32], F32, name="b_cols", tag="picked_s1", align_bytes=64)
         nc.vector.transpose(b_cols[:], b_rows[:])
-        q_w20 = dense(raw_w20, "w20", 200)
+        q_w20 = dense(raw_w20, "w20", 104)
         for m in range(M_TILES):
             multiply(m, q_w20, slice(m * P, (m + 1) * P), q_s0, True, False)
-        q_x0 = dense(raw_x0, "x0", 200)
-        q_w10 = dense(raw_w10, "w10", 200)
+        q_x0 = dense(raw_x0, "x0", 104)
+        q_w10 = dense(raw_w10, "w10", 104)
         for m in range(M_TILES):
             multiply(m, q_w10, slice(m * P, (m + 1) * P), q_x0, False, False)
-        q_w21 = dense(raw_w21, "w21", 232)
+        q_w21 = dense(raw_w21, "w21", 152)
         for m in range(M_TILES):
             multiply(m, q_w21, slice(m * P, (m + 1) * P), q_s1, False, False)
-        q_x1 = dense(raw_x1, "x1", 320)
+        q_x1 = dense(raw_x1, "x1", 256)
 
         for h in range(2):
             cuts = (128, 0) if h == 0 else (128, 128)

from contextlib import ExitStack

import concourse.mybir as mybir

K, T, S, N = 1024, 1024, 512, 512
FLOPS = 2 * N * S * 2 * K

F32 = mybir.dt.float32
BF16 = mybir.dt.bfloat16
U32 = mybir.dt.uint32
U16 = mybir.dt.uint16
U8 = mybir.dt.uint8
FP8X4 = mybir.dt.float8_e4m3fn_x4
COPY = mybir.ActivationFunctionType.Copy
RELU = mybir.ActivationFunctionType.Relu
ADD = mybir.AluOpType.add
MAX = mybir.AluOpType.max

P = 128
PACK = 4
K_PASS = P * PACK
PASSES = K // K_PASS
M_TILES = N // P


def tile_picked_recall_relu_e_kernel(tc, xT, sT, w1, w2, b, offs, out):
    nc = tc.nc
    with ExitStack() as ctx:
        keep = ctx.enter_context(tc.tile_pool(name="keep", bufs=1))
        psum = ctx.enter_context(tc.psum_pool(name="psum", bufs=1))

        offsets = keep.tile([P, S // 16], U16, name="offsets")
        b_rows = keep.tile([P, 32], F32, name="b_rows", align_bytes=64)
        nc.vector.memset(b_rows[:], 0.0)

        def load(src, c, j0, j1, c0, c1, name):
            raw = keep.tile([P, j1 - j0, c1 - c0], F32, name="raw_" + name)
            rows = src[c * K_PASS : (c + 1) * K_PASS, c0:c1].rearrange("(p j) w -> p j w", j=PACK)
            nc.sync.dma_start(out=raw[:], in_=rows[:, j0:j1, :])
            return raw

        def interleave(grouped, raw, cut):
            width = raw.shape[2]
            if cut > 0:
                nc.vector.tensor_copy(
                    out=grouped[:, :cut, :].rearrange("p (c i) j -> p c j i", i=4),
                    in_=raw[:, :, :cut].rearrange("p j (c i) -> p c j i", i=4),
                )
            if cut < width:
                nc.scalar.activation(
                    grouped[:, cut:, :].rearrange("p (c i) j -> p c j i", i=4),
                    raw[:, :, cut:].rearrange("p j (c i) -> p c j i", i=4),
                    COPY,
                )

        def quantize(grouped, name):
            width = grouped.shape[1]
            codes = keep.tile([P, width], U32, name="codes_" + name, align_bytes=64)
            scales = keep.tile([P, width], U8, name="scales_" + name, align_bytes=64)
            nc.vector.quantize_mx(
                out=codes[:].bitcast(FP8X4),
                scales=scales[:],
                in_=grouped[:].rearrange("p w j -> p (w j)"),
            )
            return codes, scales

        def dense(raw, name, cut):
            grouped = keep.tile([P, raw.shape[2], PACK], BF16, name="grouped_" + name, align_bytes=64)
            interleave(grouped, raw, cut)
            return quantize(grouped, name)

        def picked_pass(raws, name, cut, tag):
            grouped = keep.tile([P, S, PACK], BF16, name="picked_" + name, tag=tag, align_bytes=64)
            words = grouped[:].rearrange("p s j -> p (s j)").bitcast(U32).rearrange("p (s u) -> p s u", u=2)
            for u in range(2):
                pairs = keep.tile([P, T, 2], BF16, name="pairs_%s%d" % (name, u), align_bytes=64)
                interleave(pairs, raws[u], cut)
                table = pairs[:].rearrange("p t e -> p (t e)").bitcast(U32)
                nc.vector.tensor_copy(words[:, :, u], table.indirect(offsets[:]))
            return quantize(grouped, name)

        raw_s0 = [load(sT, 0, 0, 2, 0, T, "s00")]
        nc.sync.dma_start(out=offsets[:], in_=offs)
        for g in range(4):
            nc.scalar.dma_start(
                out=b_rows[32 * g : 32 * g + M_TILES, :],
                in_=b.rearrange("(c g r) o -> g c (r o)", g=4, r=32)[g],
            )
        raw_s0.append(load(sT, 0, 2, 4, 0, T, "s01"))
        raw_s1 = [load(sT, 1, 2 * u, 2 * u + 2, 0, T, "s1%d" % u) for u in range(2)]
        raw_w20 = load(w2, 0, 0, 4, 0, N, "w20")
        raw_x0 = load(xT, 0, 0, 4, 0, S, "x0")
        raw_w10 = load(w1, 0, 0, 4, 0, N, "w10")
        raw_w21 = load(w2, 1, 0, 4, 0, N, "w21")
        raw_x1 = load(xT, 1, 0, 4, 0, S, "x1")
        raw_w11 = [load(w1, 1, 0, 4, h * 256, (h + 1) * 256, "w11%d" % h) for h in range(2)]

        acc = [psum.tile([P, S], F32, name="acc%d" % m) for m in range(M_TILES)]

        def multiply(m, weights, cols, moving, start, stop):
            nc.tensor.matmul_mx(
                out=acc[m][:],
                lhsT=weights[0][:, cols].bitcast(FP8X4),
                lhsT_scale=weights[1][:, cols],
                rhs=moving[0][:].bitcast(FP8X4),
                rhs_scale=moving[1][:],
                start=start,
                stop=stop,
            )

        q_s0 = picked_pass(raw_s0, "s0", 256, "picked_s0")
        q_s1 = picked_pass(raw_s1, "s1", 256, "picked_s1")
        b_cols = keep.tile([P, 32], F32, name="b_cols", tag="picked_s1", align_bytes=64)
        nc.vector.transpose(b_cols[:], b_rows[:])
        q_w20 = dense(raw_w20, "w20", 104)
        for m in range(M_TILES):
            multiply(m, q_w20, slice(m * P, (m + 1) * P), q_s0, True, False)
        q_x0 = dense(raw_x0, "x0", 104)
        q_w10 = dense(raw_w10, "w10", 104)
        for m in range(M_TILES):
            multiply(m, q_w10, slice(m * P, (m + 1) * P), q_x0, False, False)
        q_w21 = dense(raw_w21, "w21", 152)
        for m in range(M_TILES):
            multiply(m, q_w21, slice(m * P, (m + 1) * P), q_s1, False, False)
        q_x1 = dense(raw_x1, "x1", 256)

        for h in range(2):
            cuts = (128, 0) if h == 0 else (128, 128)
            grouped = []
            for i in range(2):
                part = keep.tile([P, P, PACK], BF16, name="grouped_w11%d%d" % (h, i), align_bytes=64)
                interleave(part, raw_w11[h][:, :, i * P : (i + 1) * P], cuts[i])
                grouped.append(part)
            for i in range(2):
                m = 2 * h + i
                q_w11 = quantize(grouped[i], "w11%d%d" % (h, i))
                multiply(m, q_w11, slice(0, P), q_x1, False, True)
                result = keep.tile([P, S], F32, name="result%d" % m)
                if m != 2:
                    nc.scalar.activation(result[:], acc[m][:], RELU, bias=b_cols[:, m : m + 1])
                else:
                    nc.vector.tensor_scalar(result[:], acc[m][:], b_cols[:, m : m + 1], 0.0, ADD, MAX)
                nc.sync.dma_start(out=out[m * P : (m + 1) * P, :], in_=result[:])
